import numpy as np
import ml_dtypes


def mxq(x, axis, fmt="e4m3"):
    dtype, down = {"e4m3": (ml_dtypes.float8_e4m3fn, 7), "e5m2": (ml_dtypes.float8_e5m2, 14)}[fmt]
    v = np.moveaxis(np.asarray(x, np.float32).astype(ml_dtypes.bfloat16).astype(np.float64), axis, -1)
    blocks = v.reshape(v.shape[:-1] + (-1, 32))
    amax = np.abs(blocks).max(-1, keepdims=True)
    byte = np.maximum(np.where(amax > 0, np.frexp(amax)[1] - 1 + 127, 0) - down, 1)
    scale = np.exp2(byte - 127.0)
    codes = (blocks / scale).astype(np.float32).astype(dtype).astype(np.float64)
    return np.moveaxis((codes * scale).reshape(v.shape), -1, axis)


WIDE = False


def mx_kscale(k):
    if not WIDE:
        return np.ones(k)
    levels = np.array([10, -10, 5, -5, 0])
    if k % 512:
        return np.exp2(np.random.permutation(np.resize(levels, k // 32))).repeat(32)
    a = np.empty((k // 512, 16))
    for p in range(k // 512):
        a[p, :8] = np.random.permutation(np.resize(levels, 8))
        for g in range(8):
            far = levels[np.abs(levels - a[p, g]) >= 10]
            a[p, g + 8] = far[np.random.randint(len(far))]
    return np.exp2(a.ravel()).repeat(32)


def f64(x):
    return np.asarray(x).astype(np.float64)


def striped8(idx):
    return np.asarray(idx).reshape(8, -1, 16).transpose(0, 2, 1).reshape(128, -1).astype(np.uint16)


def unstriped8(offs):
    return offs.reshape(8, 16, -1).transpose(0, 2, 1).reshape(8, -1).astype(np.int64)


def pick8(x, idx, run):
    r = np.arange(len(x))
    return x[r[:, None], idx[r % (8 * run) // run]]


E2M1 = np.array([0.0, 0.5, 1.0, 1.5, 2.0, 3.0, 4.0, 6.0, -0.0, -0.5, -1.0, -1.5, -2.0, -3.0, -4.0, -6.0])


def pack_weight(w, fmt):
    k, n = w.shape
    w = f64(np.asarray(w, np.float32).astype(ml_dtypes.bfloat16)).reshape(k // 32, 32, n)
    amax = np.abs(w).max(1)
    if fmt == "e4m3":
        byte = np.frexp(amax)[1] - 1 + 127 - 7
    else:
        mant, ex = np.frexp(amax / 6.0)
        byte = np.where(mant > 0.5, ex, ex - 1) + 127
    byte = np.clip(np.where(amax > 0, byte, 1), 1, 254)
    scaled = (w * np.exp2(127.0 - byte)[:, None, :]).reshape(k, n).astype(np.float32)
    by_word = np.ascontiguousarray(scaled.reshape(k // 512, 128, 4, n).transpose(0, 1, 3, 2))
    if fmt == "e4m3":
        words = by_word.astype(ml_dtypes.float8_e4m3fn).view(np.uint8)
    else:
        c = by_word.astype(ml_dtypes.float4_e2m1fn).view(np.uint8) & 0xF
        words = (c[..., 0::2] | (c[..., 1::2] << 4)).reshape(k // 512, 128, 2 * n)
    return np.ascontiguousarray(words), np.ascontiguousarray(byte.astype(np.uint8).reshape(k // 512, 16, n))


def unpack_weight(words, scales, fmt):
    g, _, n = scales.shape
    words = np.ascontiguousarray(words).reshape(g, 128, n, -1)
    if fmt == "e4m3":
        vals = words.view(ml_dtypes.float8_e4m3fn).astype(np.float64)
    else:
        nib = np.empty((g, 128, n, 4), np.uint8)
        nib[..., 0::2] = words & 0xF
        nib[..., 1::2] = words >> 4
        vals = E2M1[nib]
    vals = vals * np.repeat(np.exp2(scales.astype(np.float64) - 127.0), 8, axis=1)[..., None]
    return vals.transpose(0, 1, 3, 2).reshape(g * 512, n)


def bf(x):
    return np.asarray(x, np.float32).astype(ml_dtypes.bfloat16)


def planes(Y):
    r, m = Y.shape
    b = f64(bf(Y)).reshape(r // 32, 32, m)
    amax = np.abs(b).max(1)
    byte = np.clip(np.where(amax > 0, np.frexp(amax)[1] - 1 + 127 - 7, 1), 1, 254)
    codes = (b * np.exp2(127.0 - byte)[:, None, :]).reshape(r, m).astype(np.float32).astype(ml_dtypes.float8_e4m3fn).view(np.uint8)
    words = codes.reshape(r // 512, 128, 4, m).transpose(0, 1, 3, 2)
    return np.ascontiguousarray(words), np.ascontiguousarray(byte.astype(np.uint8).reshape(r // 512, 16, m))


K, T, J, R, N = 512, 1024, 512, 512, 512


def setup_inputs():
    n = np.random.standard_normal
    idx = np.stack([np.random.permutation(T)[:J] for _ in range(8)])
    fk = mx_kscale(K)
    fr = mx_kscale(R)
    wap = pack_weight(n((K, R)) * 1 / np.sqrt(K) * fk[:, None] * fr, "e4m3")
    wbp = pack_weight(n((R, N)) * 1 / np.sqrt(R) / fr[:, None], "e2m1")
    return {
        "xt": (n((K, T)) / fk[:, None]).astype(np.float32),
        "wa_words": wap[0],
        "wa_scales": wap[1],
        "wb_words": wbp[0],
        "wb_scales": wbp[1],
        "rw": (np.random.uniform(0.5, 2.0, (1, J))).astype(np.float32),
        "offs": striped8(idx),
    }


def reference(xt, wa_words, wa_scales, wb_words, wb_scales, rw, offs):
    idx = unstriped8(offs)
    wau = unpack_weight(wa_words, wa_scales, "e4m3")
    wbu = unpack_weight(wb_words, wb_scales, "e2m1")
    xtidxq = mxq(pick8(f64(xt), idx, 64), 0, "e4m3")
    a = wau.T @ xtidxq
    hid = np.maximum(a, 0.0)
    hidq = mxq(hid, 0, "e4m3")
    p = wbu.T @ hidq
    y = p * f64(rw)
    words, scales = planes(y)
    return y, words, scales

@@ -1,0 +1,236 @@
+from contextlib import ExitStack
+
+import concourse.mybir as mybir
+from concourse.masks import make_identity
+
+K, T, J, R, N = 512, 1024, 512, 512, 512
+FLOPS = 2 * K * R * J + 2 * R * N * J
+
+F32 = mybir.dt.float32
+BF16 = mybir.dt.bfloat16
+I32 = mybir.dt.int32
+U32 = mybir.dt.uint32
+U16 = mybir.dt.uint16
+U8 = mybir.dt.uint8
+FP8X4 = mybir.dt.float8_e4m3fn_x4
+FP4X4 = mybir.dt.float4_e2m1fn_x4
+COPY = mybir.ActivationFunctionType.Copy
+RELU = mybir.ActivationFunctionType.Relu
+MULT = mybir.AluOpType.mult
+
+P = 128
+PACK = 4
+W = 128
+CHUNKS = J // W
+
+
+def tile_moe_expert_heads_two_layers_pl_kernel(
+    tc, xt, wa_words, wa_scales, wb_words, wb_scales, rw, offs, out_0, out_1, out_2
+):
+    nc = tc.nc
+    with ExitStack() as ctx:
+        sb = ctx.enter_context(tc.tile_pool(name="sb", bufs=1))
+        ps = ctx.enter_context(tc.psum_pool(name="ps", bufs=1))
+
+        def tile(name, shape, dtype):
+            return sb.tile(shape, dtype, name=name, align_bytes=64)
+
+        offsets = sb.tile([P, J // 16], U16, name="offsets")
+        x_rows = xt.rearrange("(p t) c -> p t c", t=PACK)
+
+        wa_raw = tile("wa_raw", [P, R], I32)
+        sa_raw = tile("sa_raw", [P, R], U8)
+        wb_raw = tile("wb_raw", [P, 2 * N], U8)
+        sb_raw = tile("sb_raw", [P, N], U8)
+        rw_col = tile("rw_col", [P, CHUNKS], F32)
+        nc.gpsimd.memset(sa_raw[:].bitcast(I32), 0)
+        nc.gpsimd.memset(sb_raw[:].bitcast(I32), 0)
+        ident = tile("ident", [P, P], F32)
+
+        def load_scales(queue, dst, src):
+            rows = src[0].bitcast(I32)
+            for i in range(4):
+                queue[i].dma_start(out=dst[i:P:32, :].bitcast(I32), in_=rows[i:16:4, :])
+
+        pieces = [(0, 0, 512), (0, 512, 512), (1, 0, 512), (1, 512, 256), (1, 768, 256)]
+        raws = [tile("raw%d" % n, [P, 2, w], F32) for n, (u, c0, w) in enumerate(pieces)]
+
+        def load_piece(n):
+            u, c0, w = pieces[n]
+            nc.sync.dma_start(out=raws[n][:], in_=x_rows[:, 2 * u : 2 * u + 2, c0 : c0 + w])
+
+        nc.sync.dma_start(offsets[:], offs)
+        nc.scalar.dma_start(out=rw_col[:], in_=rw.rearrange("o (p c) -> p (o c)", c=CHUNKS))
+        load_piece(0)
+        load_scales([nc.sync, nc.sync, nc.scalar, nc.scalar], sa_raw, wa_scales)
+        load_piece(1)
+        load_piece(2)
+        load_scales([nc.sync] * 4, sb_raw, wb_scales)
+        load_piece(3)
+        load_piece(4)
+        nc.sync.dma_start(out=wa_raw[:], in_=wa_words[0].rearrange("p c r -> p (c r)").bitcast(I32))
+        nc.sync.dma_start(out=wb_raw[:].bitcast(I32), in_=wb_words[0].bitcast(I32))
+        make_identity(nc, ident[:])
+
+        wa_q = tile("wa_q", [P, PACK, P], I32)
+        sa_q = tile("sa_q", [P, PACK, P], U8)
+        wb_q = tile("wb_q", [P, PACK, 2 * P], U8)
+        sb_q = tile("sb_q", [P, PACK, P], U8)
+        nc.gpsimd.tensor_copy(out=sb_q[:], in_=sb_raw[:].rearrange("p (m t) -> p t m", t=PACK))
+        nc.vector.tensor_copy(out=sa_q[:], in_=sa_raw[:].rearrange("p (m t) -> p t m", t=PACK))
+
+        pairs = [tile("pairs%d" % u, [P, T], U32) for u in range(2)]
+
+        def cast(n, lo, hi, on_scalar):
+            u, c0, w = pieces[n]
+            dst = pairs[u][:, c0 + lo : c0 + hi].bitcast(BF16).rearrange("p (c e) -> p c e", e=2)
+            src = raws[n][:, :, lo:hi].rearrange("p e c -> p c e")
+            if on_scalar:
+                nc.scalar.activation(out=dst, in_=src, func=COPY)
+            else:
+                nc.vector.tensor_copy(out=dst, in_=src)
+
+        shared = tile("picked_shared", [P, 4, W], U32)
+        picked = [shared[:, 2:4, :], tile("picked1", [P, 2, W], U32)[:], shared[:, 0:4:3, :], shared[:, 1:3, :]]
+        xg = [tile("xg%d" % c, [P, W, 2], U32) for c in range(CHUNKS)]
+        xq = [tile("xq%d" % c, [P, W], U32) for c in range(CHUNKS)]
+        xs = [tile("xs%d" % c, [P, W], U8) for c in range(CHUNKS)]
+        hg = [tile("hg%d" % c, [P, W, PACK], BF16) for c in range(CHUNKS)]
+        hq = [tile("hq%d" % c, [P, W], U32) for c in range(CHUNKS)]
+        hs = [tile("hs%d" % c, [P, W], U8) for c in range(CHUNKS)]
+        y = [tile("y%d" % c, [P, PACK, W], F32) for c in range(CHUNKS)]
+        yg = [tile("yg%d" % c, [P, W, PACK], BF16) for c in range(CHUNKS)]
+        yq = tile("yq", [P, J], U32)
+        ys = tile("ys", [P, J], U8)
+        rw_all = tile("rw_all", [P, J], F32)
+
+        def gather(u, c):
+            nc.vector.tensor_copy(picked[c][:, u, :], pairs[u][:].indirect(offsets[:, 8 * c : 8 * c + 8]))
+
+        def weave(c, on_scalar):
+            src = picked[c].rearrange("p u j -> p j u")
+            if on_scalar:
+                nc.scalar.copy(out=xg[c][:], in_=src)
+            else:
+                nc.vector.tensor_copy(out=xg[c][:].bitcast(I32), in_=picked[c].bitcast(I32).rearrange("p u j -> p j u"))
+
+        def quant_x(c):
+            nc.vector.quantize_mx(out=xq[c][:].bitcast(FP8X4), scales=xs[c][:],
+                                  in_=xg[c][:].rearrange("p j u -> p (j u)").bitcast(BF16))
+
+        a_ps = {}
+        p_ps = {}
+
+        def layer1(c):
+            a_ps[c] = ps.tile([P, PACK, W], F32, name="a%d" % c, tag="a", bufs=4)
+            for t in range(PACK):
+                nc.tensor.matmul_mx(out=a_ps[c][:, t, :], lhsT=wa_q[:, t, :].bitcast(FP8X4), lhsT_scale=sa_q[:, t, :],
+                                    rhs=xq[c][:].bitcast(FP8X4), rhs_scale=xs[c][:], start=True, stop=True)
+
+        def relu(c, on_scalar):
+            src = a_ps[c][:].rearrange("p t j -> p j t")
+            if on_scalar:
+                nc.scalar.activation(out=hg[c][:], in_=src, func=RELU)
+            else:
+                nc.vector.tensor_scalar_max(out=hg[c][:], in0=src, scalar1=0.0)
+
+        def quant_h(c):
+            nc.vector.quantize_mx(out=hq[c][:].bitcast(FP8X4), scales=hs[c][:],
+                                  in_=hg[c][:].rearrange("p j t -> p (j t)"))
+
+        def layer2(c):
+            p_ps[c] = ps.tile([P, PACK, W], F32, name="p%d" % c, tag="p", bufs=4)
+            for t in range(PACK):
+                nc.tensor.matmul_mx(out=p_ps[c][:, t, :], lhsT=wb_q[:, t, :].bitcast(FP4X4), lhsT_scale=sb_q[:, t, :],
+                                    rhs=hq[c][:].bitcast(FP8X4), rhs_scale=hs[c][:], start=True, stop=True)
+
+        out_rows = out_0.rearrange("(p t) j -> p t j", t=PACK)
+        out_words = out_1[0].rearrange("p c r -> p (c r)").bitcast(I32)
+
+        def weigh(c):
+            gate = rw_all[:, W * c : W * (c + 1)].unsqueeze(1).to_broadcast([P, PACK, W])
+            nc.vector.tensor_tensor(out=y[c][:], in0=p_ps[c][:], in1=gate, op=MULT)
+            nc.sync.dma_start(out=out_rows[:, :, W * c : W * (c + 1)], in_=y[c][:])
+
+        def round_y(c, on_scalar):
+            src = y[c][:].rearrange("p t j -> p j t")
+            if on_scalar:
+                nc.scalar.activation(out=yg[c][:], in_=src, func=COPY)
+            else:
+                nc.vector.tensor_copy(out=yg[c][:], in_=src)
+
+        def quant_y(c):
+            cols = slice(W * c, W * (c + 1))
+            nc.vector.quantize_mx(out=yq[:, cols].bitcast(FP8X4), scales=ys[:, cols],
+                                  in_=yg[c][:].rearrange("p j t -> p (j t)"))
+
+        rw_ps = ps.tile([P, CHUNKS, P], F32, name="rw_ps", tag="p", bufs=4)
+        for c in range(CHUNKS):
+            nc.tensor.transpose(rw_ps[:, c, :], rw_col[:, c : c + 1].to_broadcast([P, P]), ident[:])
+        nc.scalar.activation(out=rw_all[:].rearrange("q (p c) -> q p c", c=CHUNKS),
+                             in_=rw_ps[:].rearrange("q c p -> q p c"), func=COPY)
+        cast(0, 0, 256, False)
+        cast(0, 256, 512, True)
+        cast(1, 0, 320, False)
+        cast(1, 320, 512, True)
+        for c in range(CHUNKS):
+            gather(0, c)
+        cast(2, 0, 512, True)
+        cast(3, 0, 256, False)
+        cast(4, 0, 160, False)
+        cast(4, 160, 256, True)
+
+        gather(1, 0)
+        weave(0, True)
+        gather(1, 1)
+        weave(1, True)
+        nc.vector.tensor_copy(out=wa_q[:], in_=wa_raw[:].rearrange("p (m t) -> p t m", t=PACK))
+        warm_ps = ps.tile([P, R], F32, name="warm_ps", tag="p", bufs=4)
+        for n in range(2):
+            nc.tensor.matmul_mx(out=warm_ps[:], lhsT=wa_raw[:, 0:P].bitcast(FP8X4), lhsT_scale=sa_raw[:, 0:P],
+                                rhs=wa_raw[:].bitcast(FP8X4), rhs_scale=sa_raw[:], start=True, stop=True)
+        quant_x(0)
+        layer1(0)
+        gather(1, 2)
+        weave(2, True)
+        gather(1, 3)
+        weave(3, True)
+        quant_x(1)
+        layer1(1)
+        nc.vector.tensor_copy(out=wb_q[:].rearrange("p t b -> p (t b)").bitcast(U16).rearrange("p (t m) -> p t m", t=PACK),
+                              in_=wb_raw[:].bitcast(U16).rearrange("p (m t) -> p t m", t=PACK))
+        relu(0, True)
+        quant_x(2)
+        layer1(2)
+        quant_x(3)
+        quant_h(0)
+        layer2(0)
+        layer1(3)
+        relu(1, True)
+        quant_h(1)
+        weigh(0)
+        layer2(1)
+        relu(2, True)
+        quant_h(2)
+        layer2(2)
+        relu(3, True)
+        quant_h(3)
+        layer2(3)
+        weigh(1)
+        round_y(0, True)
+        weigh(2)
+        quant_y(0)
+        round_y(1, True)
+        weigh(3)
+        quant_y(1)
+        round_y(2, True)
+        round_y(3, False)
+        quant_y(2)
+        nc.sync.dma_start(out=out_words[:, 0 : 3 * W], in_=yq[:, 0 : 3 * W].bitcast(I32))
+        quant_y(3)
+        last = slice(W * (CHUNKS - 1), J)
+        nc.sync.dma_start(out=out_words[:, last], in_=yq[:, last].bitcast(I32))
+        scale_rows = out_2[0].bitcast(I32)
+        for i in range(4):
+            queue = nc.sync if i % 2 else nc.scalar
+            queue.dma_start(out=scale_rows[i:16:4, :], in_=ys[i:P:32, :].bitcast(I32))

@@ -65,8 +65,8 @@ def tile_moe_expert_heads_two_layers_pl_kernel(
         load_scales([nc.sync, nc.sync, nc.scalar, nc.scalar], sa_raw, wa_scales)
         load_piece(1)
         load_piece(2)
-        load_scales([nc.sync] * 4, sb_raw, wb_scales)
         load_piece(3)
+        load_scales([nc.sync] * 4, sb_raw, wb_scales)
         load_piece(4)
         nc.sync.dma_start(out=wa_raw[:], in_=wa_words[0].rearrange("p c r -> p (c r)").bitcast(I32))
         nc.sync.dma_start(out=wb_raw[:].bitcast(I32), in_=wb_words[0].bitcast(I32))
@@ -76,8 +76,7 @@ def tile_moe_expert_heads_two_layers_pl_kernel(
         sa_q = tile("sa_q", [P, PACK, P], U8)
         wb_q = tile("wb_q", [P, PACK, 2 * P], U8)
         sb_q = tile("sb_q", [P, PACK, P], U8)
-        nc.gpsimd.tensor_copy(out=sb_q[:], in_=sb_raw[:].rearrange("p (m t) -> p t m", t=PACK))
-        nc.vector.tensor_copy(out=sa_q[:], in_=sa_raw[:].rearrange("p (m t) -> p t m", t=PACK))
+        nc.vector.tensor_copy(out=sa_q[:].rearrange("p t m -> p m t"), in_=sa_raw[:].rearrange("p (m t) -> p m t", t=PACK))
 
         pairs = [tile("pairs%d" % u, [P, T], U32) for u in range(2)]
 
@@ -152,12 +151,13 @@ def tile_moe_expert_heads_two_layers_pl_kernel(
             nc.vector.tensor_tensor(out=y[c][:], in0=p_ps[c][:], in1=gate, op=MULT)
             nc.sync.dma_start(out=out_rows[:, :, W * c : W * (c + 1)], in_=y[c][:])
 
-        def round_y(c, on_scalar):
-            src = y[c][:].rearrange("p t j -> p j t")
+        def round_y(c, on_scalar, lo=0, hi=W):
+            src = y[c][:, :, lo:hi].rearrange("p t (g i) -> p g t i", i=4)
+            dst = yg[c][:, lo:hi, :].rearrange("p (g i) t -> p g t i", i=4)
             if on_scalar:
-                nc.scalar.activation(out=yg[c][:], in_=src, func=COPY)
+                nc.scalar.activation(out=dst, in_=src, func=COPY)
             else:
-                nc.vector.tensor_copy(out=yg[c][:], in_=src)
+                nc.vector.tensor_copy(out=dst, in_=src)
 
         def quant_y(c):
             cols = slice(W * c, W * (c + 1))
@@ -184,7 +184,7 @@ def tile_moe_expert_heads_two_layers_pl_kernel(
         weave(0, True)
         gather(1, 1)
         weave(1, True)
-        nc.vector.tensor_copy(out=wa_q[:], in_=wa_raw[:].rearrange("p (m t) -> p t m", t=PACK))
+        nc.vector.tensor_copy(out=wa_q[:].rearrange("p t m -> p m t"), in_=wa_raw[:].rearrange("p (m t) -> p m t", t=PACK))
         warm_ps = ps.tile([P, R], F32, name="warm_ps", tag="p", bufs=4)
         for n in range(2):
             nc.tensor.matmul_mx(out=warm_ps[:], lhsT=wa_raw[:, 0:P].bitcast(FP8X4), lhsT_scale=sa_raw[:, 0:P],
@@ -197,8 +197,9 @@ def tile_moe_expert_heads_two_layers_pl_kernel(
         weave(3, True)
         quant_x(1)
         layer1(1)
-        nc.vector.tensor_copy(out=wb_q[:].rearrange("p t b -> p (t b)").bitcast(U16).rearrange("p (t m) -> p t m", t=PACK),
-                              in_=wb_raw[:].bitcast(U16).rearrange("p (m t) -> p t m", t=PACK))
+        nc.vector.tensor_copy(out=wb_q[:].rearrange("p t b -> p (t b)").bitcast(U16).rearrange("p (t m) -> p m t", t=PACK),
+                              in_=wb_raw[:].bitcast(U16).rearrange("p (m t) -> p m t", t=PACK))
+        nc.vector.tensor_copy(out=sb_q[:].rearrange("p t m -> p m t"), in_=sb_raw[:].rearrange("p (m t) -> p m t", t=PACK))
         relu(0, True)
         quant_x(2)
         layer1(2)
@@ -224,7 +225,8 @@ def tile_moe_expert_heads_two_layers_pl_kernel(
         weigh(3)
         quant_y(1)
         round_y(2, True)
-        round_y(3, False)
+        round_y(3, False, 0, 80)
+        round_y(3, True, 80, W)
         quant_y(2)
         nc.sync.dma_start(out=out_words[:, 0 : 3 * W], in_=yq[:, 0 : 3 * W].bitcast(I32))
         quant_y(3)

from contextlib import ExitStack

import concourse.mybir as mybir
from concourse.masks import make_identity

K, T, J, R, N = 512, 1024, 512, 512, 512
FLOPS = 2 * K * R * J + 2 * R * N * J

F32 = mybir.dt.float32
BF16 = mybir.dt.bfloat16
I32 = mybir.dt.int32
U32 = mybir.dt.uint32
U16 = mybir.dt.uint16
U8 = mybir.dt.uint8
FP8X4 = mybir.dt.float8_e4m3fn_x4
FP4X4 = mybir.dt.float4_e2m1fn_x4
COPY = mybir.ActivationFunctionType.Copy
RELU = mybir.ActivationFunctionType.Relu
MULT = mybir.AluOpType.mult

P = 128
PACK = 4
W = 128
CHUNKS = J // W


def tile_moe_expert_heads_two_layers_pl_kernel(
    tc, xt, wa_words, wa_scales, wb_words, wb_scales, rw, offs, out_0, out_1, out_2
):
    nc = tc.nc
    with ExitStack() as ctx:
        sb = ctx.enter_context(tc.tile_pool(name="sb", bufs=1))
        ps = ctx.enter_context(tc.psum_pool(name="ps", bufs=1))

        def tile(name, shape, dtype):
            return sb.tile(shape, dtype, name=name, align_bytes=64)

        offsets = sb.tile([P, J // 16], U16, name="offsets")
        x_rows = xt.rearrange("(p t) c -> p t c", t=PACK)

        wa_raw = tile("wa_raw", [P, R], I32)
        sa_raw = tile("sa_raw", [P, R], U8)
        wb_raw = tile("wb_raw", [P, 2 * N], U8)
        sb_raw = tile("sb_raw", [P, N], U8)
        rw_col = tile("rw_col", [P, CHUNKS], F32)
        nc.gpsimd.memset(sa_raw[:].bitcast(I32), 0)
        nc.gpsimd.memset(sb_raw[:].bitcast(I32), 0)
        ident = tile("ident", [P, P], F32)

        def load_scales(queue, dst, src):
            rows = src[0].bitcast(I32)
            for i in range(4):
                queue[i].dma_start(out=dst[i:P:32, :].bitcast(I32), in_=rows[i:16:4, :])

        pieces = [(0, 0, 512), (0, 512, 512), (1, 0, 512), (1, 512, 256), (1, 768, 256)]
        raws = [tile("raw%d" % n, [P, 2, w], F32) for n, (u, c0, w) in enumerate(pieces)]

        def load_piece(n):
            u, c0, w = pieces[n]
            nc.sync.dma_start(out=raws[n][:], in_=x_rows[:, 2 * u : 2 * u + 2, c0 : c0 + w])

        nc.sync.dma_start(offsets[:], offs)
        nc.scalar.dma_start(out=rw_col[:], in_=rw.rearrange("o (p c) -> p (o c)", c=CHUNKS))
        load_piece(0)
        load_scales([nc.sync, nc.sync, nc.scalar, nc.scalar], sa_raw, wa_scales)
        load_piece(1)
        load_piece(2)
        load_piece(3)
        load_scales([nc.sync] * 4, sb_raw, wb_scales)
        load_piece(4)
        nc.sync.dma_start(out=wa_raw[:], in_=wa_words[0].rearrange("p c r -> p (c r)").bitcast(I32))
        nc.sync.dma_start(out=wb_raw[:].bitcast(I32), in_=wb_words[0].bitcast(I32))
        make_identity(nc, ident[:])

        wa_q = tile("wa_q", [P, PACK, P], I32)
        sa_q = tile("sa_q", [P, PACK, P], U8)
        wb_q = tile("wb_q", [P, PACK, 2 * P], U8)
        sb_q = tile("sb_q", [P, PACK, P], U8)
        nc.vector.tensor_copy(out=sa_q[:].rearrange("p t m -> p m t"), in_=sa_raw[:].rearrange("p (m t) -> p m t", t=PACK))

        pairs = [tile("pairs%d" % u, [P, T], U32) for u in range(2)]

        def cast(n, lo, hi, on_scalar):
            u, c0, w = pieces[n]
            dst = pairs[u][:, c0 + lo : c0 + hi].bitcast(BF16).rearrange("p (c e) -> p c e", e=2)
            src = raws[n][:, :, lo:hi].rearrange("p e c -> p c e")
            if on_scalar:
                nc.scalar.activation(out=dst, in_=src, func=COPY)
            else:
                nc.vector.tensor_copy(out=dst, in_=src)

        shared = tile("picked_shared", [P, 4, W], U32)
        picked = [shared[:, 2:4, :], tile("picked1", [P, 2, W], U32)[:], shared[:, 0:4:3, :], shared[:, 1:3, :]]
        xg = [tile("xg%d" % c, [P, W, 2], U32) for c in range(CHUNKS)]
        xq = [tile("xq%d" % c, [P, W], U32) for c in range(CHUNKS)]
        xs = [tile("xs%d" % c, [P, W], U8) for c in range(CHUNKS)]
        hg = [tile("hg%d" % c, [P, W, PACK], BF16) for c in range(CHUNKS)]
        hq = [tile("hq%d" % c, [P, W], U32) for c in range(CHUNKS)]
        hs = [tile("hs%d" % c, [P, W], U8) for c in range(CHUNKS)]
        y = [tile("y%d" % c, [P, PACK, W], F32) for c in range(CHUNKS)]
        yg = [tile("yg%d" % c, [P, W, PACK], BF16) for c in range(CHUNKS)]
        yq = tile("yq", [P, J], U32)
        ys = tile("ys", [P, J], U8)
        rw_all = tile("rw_all", [P, J], F32)

        def gather(u, c):
            nc.vector.tensor_copy(picked[c][:, u, :], pairs[u][:].indirect(offsets[:, 8 * c : 8 * c + 8]))

        def weave(c, on_scalar):
            src = picked[c].rearrange("p u j -> p j u")
            if on_scalar:
                nc.scalar.copy(out=xg[c][:], in_=src)
            else:
                nc.vector.tensor_copy(out=xg[c][:].bitcast(I32), in_=picked[c].bitcast(I32).rearrange("p u j -> p j u"))

        def quant_x(c):
            nc.vector.quantize_mx(out=xq[c][:].bitcast(FP8X4), scales=xs[c][:],
                                  in_=xg[c][:].rearrange("p j u -> p (j u)").bitcast(BF16))

        a_ps = {}
        p_ps = {}

        def layer1(c):
            a_ps[c] = ps.tile([P, PACK, W], F32, name="a%d" % c, tag="a", bufs=4)
            for t in range(PACK):
                nc.tensor.matmul_mx(out=a_ps[c][:, t, :], lhsT=wa_q[:, t, :].bitcast(FP8X4), lhsT_scale=sa_q[:, t, :],
                                    rhs=xq[c][:].bitcast(FP8X4), rhs_scale=xs[c][:], start=True, stop=True)

        def relu(c, on_scalar):
            src = a_ps[c][:].rearrange("p t j -> p j t")
            if on_scalar:
                nc.scalar.activation(out=hg[c][:], in_=src, func=RELU)
            else:
                nc.vector.tensor_scalar_max(out=hg[c][:], in0=src, scalar1=0.0)

        def quant_h(c):
            nc.vector.quantize_mx(out=hq[c][:].bitcast(FP8X4), scales=hs[c][:],
                                  in_=hg[c][:].rearrange("p j t -> p (j t)"))

        def layer2(c):
            p_ps[c] = ps.tile([P, PACK, W], F32, name="p%d" % c, tag="p", bufs=4)
            for t in range(PACK):
                nc.tensor.matmul_mx(out=p_ps[c][:, t, :], lhsT=wb_q[:, t, :].bitcast(FP4X4), lhsT_scale=sb_q[:, t, :],
                                    rhs=hq[c][:].bitcast(FP8X4), rhs_scale=hs[c][:], start=True, stop=True)

        out_rows = out_0.rearrange("(p t) j -> p t j", t=PACK)
        out_words = out_1[0].rearrange("p c r -> p (c r)").bitcast(I32)

        def weigh(c):
            gate = rw_all[:, W * c : W * (c + 1)].unsqueeze(1).to_broadcast([P, PACK, W])
            nc.vector.tensor_tensor(out=y[c][:], in0=p_ps[c][:], in1=gate, op=MULT)
            nc.sync.dma_start(out=out_rows[:, :, W * c : W * (c + 1)], in_=y[c][:])

        def round_y(c, on_scalar, lo=0, hi=W):
            src = y[c][:, :, lo:hi].rearrange("p t (g i) -> p g t i", i=4)
            dst = yg[c][:, lo:hi, :].rearrange("p (g i) t -> p g t i", i=4)
            if on_scalar:
                nc.scalar.activation(out=dst, in_=src, func=COPY)
            else:
                nc.vector.tensor_copy(out=dst, in_=src)

        def quant_y(c):
            cols = slice(W * c, W * (c + 1))
            nc.vector.quantize_mx(out=yq[:, cols].bitcast(FP8X4), scales=ys[:, cols],
                                  in_=yg[c][:].rearrange("p j t -> p (j t)"))

        rw_ps = ps.tile([P, CHUNKS, P], F32, name="rw_ps", tag="p", bufs=4)
        for c in range(CHUNKS):
            nc.tensor.transpose(rw_ps[:, c, :], rw_col[:, c : c + 1].to_broadcast([P, P]), ident[:])
        nc.scalar.activation(out=rw_all[:].rearrange("q (p c) -> q p c", c=CHUNKS),
                             in_=rw_ps[:].rearrange("q c p -> q p c"), func=COPY)
        cast(0, 0, 256, False)
        cast(0, 256, 512, True)
        cast(1, 0, 320, False)
        cast(1, 320, 512, True)
        for c in range(CHUNKS):
            gather(0, c)
        cast(2, 0, 512, True)
        cast(3, 0, 256, False)
        cast(4, 0, 160, False)
        cast(4, 160, 256, True)

        gather(1, 0)
        weave(0, True)
        gather(1, 1)
        weave(1, True)
        nc.vector.tensor_copy(out=wa_q[:].rearrange("p t m -> p m t"), in_=wa_raw[:].rearrange("p (m t) -> p m t", t=PACK))
        warm_ps = ps.tile([P, R], F32, name="warm_ps", tag="p", bufs=4)
        for n in range(2):
            nc.tensor.matmul_mx(out=warm_ps[:], lhsT=wa_raw[:, 0:P].bitcast(FP8X4), lhsT_scale=sa_raw[:, 0:P],
                                rhs=wa_raw[:].bitcast(FP8X4), rhs_scale=sa_raw[:], start=True, stop=True)
        quant_x(0)
        layer1(0)
        gather(1, 2)
        weave(2, True)
        gather(1, 3)
        weave(3, True)
        quant_x(1)
        layer1(1)
        nc.vector.tensor_copy(out=wb_q[:].rearrange("p t b -> p (t b)").bitcast(U16).rearrange("p (t m) -> p m t", t=PACK),
                              in_=wb_raw[:].bitcast(U16).rearrange("p (m t) -> p m t", t=PACK))
        nc.vector.tensor_copy(out=sb_q[:].rearrange("p t m -> p m t"), in_=sb_raw[:].rearrange("p (m t) -> p m t", t=PACK))
        relu(0, True)
        quant_x(2)
        layer1(2)
        quant_x(3)
        quant_h(0)
        layer2(0)
        layer1(3)
        relu(1, True)
        quant_h(1)
        weigh(0)
        layer2(1)
        relu(2, True)
        quant_h(2)
        layer2(2)
        relu(3, True)
        quant_h(3)
        layer2(3)
        weigh(1)
        round_y(0, True)
        weigh(2)
        quant_y(0)
        round_y(1, True)
        weigh(3)
        quant_y(1)
        round_y(2, True)
        round_y(3, False, 0, 80)
        round_y(3, True, 80, W)
        quant_y(2)
        nc.sync.dma_start(out=out_words[:, 0 : 3 * W], in_=yq[:, 0 : 3 * W].bitcast(I32))
        quant_y(3)
        last = slice(W * (CHUNKS - 1), J)
        nc.sync.dma_start(out=out_words[:, last], in_=yq[:, last].bitcast(I32))
        scale_rows = out_2[0].bitcast(I32)
        for i in range(4):
            queue = nc.sync if i % 2 else nc.scalar
            queue.dma_start(out=scale_rows[i:16:4, :], in_=ys[i:P:32, :].bitcast(I32))
